import numpy as np
import ml_dtypes


def mxq(x, axis, fmt="e4m3"):
    dtype, down = {"e4m3": (ml_dtypes.float8_e4m3fn, 7), "e5m2": (ml_dtypes.float8_e5m2, 14)}[fmt]
    v = np.moveaxis(np.asarray(x, np.float32).astype(ml_dtypes.bfloat16).astype(np.float64), axis, -1)
    blocks = v.reshape(v.shape[:-1] + (-1, 32))
    amax = np.abs(blocks).max(-1, keepdims=True)
    byte = np.maximum(np.where(amax > 0, np.frexp(amax)[1] - 1 + 127, 0) - down, 1)
    scale = np.exp2(byte - 127.0)
    codes = (blocks / scale).astype(np.float32).astype(dtype).astype(np.float64)
    return np.moveaxis((codes * scale).reshape(v.shape), -1, axis)


WIDE = False


def mx_kscale(k):
    if not WIDE:
        return np.ones(k)
    levels = np.array([10, -10, 5, -5, 0])
    if k % 512:
        return np.exp2(np.random.permutation(np.resize(levels, k // 32))).repeat(32)
    a = np.empty((k // 512, 16))
    for p in range(k // 512):
        a[p, :8] = np.random.permutation(np.resize(levels, 8))
        for g in range(8):
            far = levels[np.abs(levels - a[p, g]) >= 10]
            a[p, g + 8] = far[np.random.randint(len(far))]
    return np.exp2(a.ravel()).repeat(32)


def f64(x):
    return np.asarray(x).astype(np.float64)


def striped(idx):
    return np.tile(idx.reshape(-1, 16).T, (8, 1)).astype(np.uint16)


def unstriped(offs):
    return offs[:16].T.reshape(-1).astype(np.int64)


def pack_weight(w):
    k, n = w.shape
    w = f64(np.asarray(w, np.float32).astype(ml_dtypes.bfloat16)).reshape(k // 32, 32, n)
    amax = np.abs(w).max(1)
    byte = np.clip(np.where(amax > 0, np.frexp(amax)[1] - 1 + 127 - 7, 1), 1, 254)
    scaled = (w * np.exp2(127.0 - byte)[:, None, :]).reshape(k, n).astype(np.float32)
    words = np.ascontiguousarray(scaled.reshape(k // 512, 128, 4, n).transpose(0, 1, 3, 2)).astype(ml_dtypes.float8_e4m3fn).view(np.uint8)
    return words, np.ascontiguousarray(byte.astype(np.uint8).reshape(k // 512, 16, n))


def unpack_weight(words, scales):
    g, p, n, _ = words.shape
    vals = np.ascontiguousarray(words).view(ml_dtypes.float8_e4m3fn).astype(np.float64) * np.repeat(np.exp2(scales.astype(np.float64) - 127.0), 8, axis=1)[..., None]
    return vals.transpose(0, 1, 3, 2).reshape(g * 512, n)


K, T, S, N, H, U = 512, 1024, 512, 128, 512, 1024


def setup_inputs():
    n = np.random.standard_normal
    s = mx_kscale(K)[:, None]
    u = mx_kscale(H)
    packed_xT = pack_weight(n((K, T)) * s)
    return {
        "x_words": packed_xT[0],
        "x_scales": packed_xT[1],
        "w1": (n((K, H)) / np.sqrt(K) / s).astype(np.float32),
        "w2": (n((K, H)) / np.sqrt(K) / s).astype(np.float32),
        "dist": (np.random.uniform(0.6, 2.5, (H, U))).astype(np.float32),
        "unit": (np.random.uniform(0.6, 1.4, (H, 1)) * u[:, None]).astype(np.float32),
        "w3": (n((H, N)) / np.sqrt(H) / u[:, None]).astype(np.float32),
        "offs": striped(np.random.permutation(T)[:S]),
        "pi": striped(np.random.permutation(np.concatenate([np.arange(S), np.random.randint(0, S, U - S)]))),
        "pj": striped(np.random.permutation(np.concatenate([np.arange(S), np.random.randint(0, S, U - S)]))),
    }


def reference(x_words, x_scales, w1, w2, dist, unit, w3, offs, pi, pj):
    xq = unpack_weight(x_words, x_scales)[:, unstriped(offs)]
    chg = mxq(f64(w1), 0, "e4m3").T @ xq
    qi = chg[:, unstriped(pi)]
    qj = chg[:, unstriped(pj)]
    damp = (np.exp(-1.0 * ((0.8 * f64(dist)) ** 2))) / f64(dist)
    cou = (qi * qj) * damp
    pol = mxq(f64(w2), 0, "e4m3").T @ xq
    alpha = np.log(np.exp(pol) + 1.0)
    al_i = alpha[:, unstriped(pi)]
    alij = np.sqrt(al_i * alpha[:, unstriped(pj)] + 0.1)
    ind = (((qi) ** 2) * alij) * (damp / f64(dist))
    hid = f64(unit) * (cou - (0.5 * ind))
    return mxq(f64(w3), 0, "e4m3").T @ mxq(hid, 0, "e4m3")

@@ -1,0 +1,277 @@
+from contextlib import ExitStack
+
+import concourse.mybir as mybir
+
+K, T, S, N, H, U = 512, 1024, 512, 128, 512, 1024
+FLOPS = 2 * K * H * S * 2 + 2 * H * N * U
+
+F32 = mybir.dt.float32
+BF16 = mybir.dt.bfloat16
+I32 = mybir.dt.int32
+U32 = mybir.dt.uint32
+U16 = mybir.dt.uint16
+U8 = mybir.dt.uint8
+FP8X4 = mybir.dt.float8_e4m3fn_x4
+ACT = mybir.ActivationFunctionType
+ALU = mybir.AluOpType
+
+P = 128
+PACK = 4
+CHUNKS = (256, 256, 256, 256)
+WINDOW = U + 32
+
+
+def tile_picked_yewald_pol_p_kernel(
+    tc, x_words, x_scales, w1, w2, dist, unit, w3, offs, pi, pj, out
+):
+    nc = tc.nc
+    with ExitStack() as ctx:
+        keep = ctx.enter_context(tc.tile_pool(name="keep", bufs=1))
+        ring = ctx.enter_context(tc.tile_pool(name="ring", bufs=3))
+        psum = ctx.enter_context(tc.psum_pool(name="psum", bufs=4))
+
+        offs_sb = keep.tile([P, S // 16], U16, name="offs_sb")
+        pi_sb = keep.tile([P, U // 16], U16, name="pi_sb")
+        pj_sb = keep.tile([P, U // 16], U16, name="pj_sb")
+
+        table_scales = keep.tile([P, T], U8, name="table_scales", align_bytes=64)
+        nc.vector.memset(table_scales[:].bitcast(I32), 0)
+        for q in range(4):
+            nc.scalar.dma_start(
+                out=table_scales[32 * q : 32 * q + 4, :].bitcast(I32),
+                in_=x_scales[0, 4 * q : 4 * q + 4, :].bitcast(I32),
+            )
+
+        dist_rows = dist.rearrange("(p t) r -> t p r", t=PACK)
+        d = []
+        for t in range(PACK):
+            d_t = keep.tile([P, U], F32, name="d%d" % t)
+            nc.sync.dma_start(out=d_t[:], in_=dist_rows[t])
+            d.append(d_t)
+
+        table_words = keep.tile([P, T], U32, name="table_words", align_bytes=64)
+        nc.sync.dma_start(
+            out=table_words[:].bitcast(I32),
+            in_=x_words[0].rearrange("p n t -> p (n t)").bitcast(I32),
+        )
+        nc.sync.dma_start(offs_sb[:], offs)
+
+        def load_halves(w, name):
+            rows = w.rearrange("(p j) c -> p j c", j=PACK)
+            halves = []
+            for h in range(2):
+                raw = keep.tile([P, PACK, H // 2], F32, name="%s_raw%d" % (name, h))
+                nc.sync.dma_start(out=raw[:], in_=rows[:, :, h * (H // 2) : (h + 1) * (H // 2)])
+                halves.append(raw)
+            return halves
+
+        w1_raw = load_halves(w1, "w1")
+        nc.sync.dma_start(pi_sb[:], pi)
+        w2_raw = load_halves(w2, "w2")
+        nc.sync.dma_start(pj_sb[:], pj)
+        unit_sb = keep.tile([P, PACK], F32, name="unit_sb")
+        nc.sync.dma_start(out=unit_sb[:], in_=unit.rearrange("(p t) o -> p (t o)", t=PACK))
+        w3_raw = keep.tile([P, PACK, N], F32, name="w3_raw")
+        nc.sync.dma_start(out=w3_raw[:], in_=w3.rearrange("(p j) c -> p j c", j=PACK))
+
+        gauss = keep.tile([P, PACK, U], F32, name="gauss")
+        inv_d = keep.tile([P, PACK, U], F32, name="inv_d")
+        for t in range(PACK):
+            nc.vector.tensor_tensor(gauss[:, t, :], d[t][:], d[t][:], ALU.mult)
+            nc.scalar.activation(inv_d[:, t, :], gauss[:, t, :], ACT.Abs_reciprocal_sqrt)
+
+        x_codes = keep.tile([P, S], U32, name="x_codes", align_bytes=64)
+        x_sc = keep.tile([P, S], U8, name="x_sc", align_bytes=64)
+        nc.vector.tensor_copy(x_codes[:], table_words[:].indirect(offs_sb[:]))
+        nc.vector.tensor_copy(x_sc[:], table_scales[:].indirect(offs_sb[:]))
+
+        def product(halves, name):
+            grouped = keep.tile([P, PACK, P, PACK], BF16, name=name + "_grouped", align_bytes=64)
+            codes = keep.tile([P, H], U32, name=name + "_codes", align_bytes=64)
+            scales = keep.tile([P, H], U8, name=name + "_scales", align_bytes=64)
+            for h in range(2):
+                nc.vector.tensor_copy(
+                    grouped[:, :, h * (P // 2) : (h + 1) * (P // 2), :].rearrange("p t m j -> p m j t"),
+                    halves[h][:].rearrange("p j (m t) -> p m j t", t=PACK),
+                )
+            banks = []
+            for t in range(PACK):
+                cols = slice(t * P, (t + 1) * P)
+                nc.vector.quantize_mx(
+                    out=codes[:, cols].bitcast(FP8X4),
+                    scales=scales[:, cols],
+                    in_=grouped[:, t, :, :].rearrange("p m j -> p (m j)"),
+                )
+                bank = psum.tile([P, S], F32, name=name + "_bank", tag=name + "_bank")
+                nc.tensor.matmul_mx(
+                    out=bank[:],
+                    lhsT=codes[:, cols].bitcast(FP8X4),
+                    lhsT_scale=scales[:, cols],
+                    rhs=x_codes[:].bitcast(FP8X4),
+                    rhs_scale=x_sc[:],
+                    start=True,
+                    stop=True,
+                )
+                banks.append(bank)
+            return banks
+
+        chg_banks = product(w1_raw, "w1")
+        chg = []
+        for t in range(PACK):
+            chg_t = keep.tile([P, WINDOW], F32, name="chg%d" % t)
+            nc.scalar.copy(chg_t[:, :S], chg_banks[t][:])
+            chg.append(chg_t)
+        pol_banks = product(w2_raw, "w2")
+
+        for h in range(2):
+            part = gauss[:, :, h * (U // 2) : (h + 1) * (U // 2)]
+            nc.scalar.activation(part, part, ACT.Exp, scale=-0.64)
+
+        qi_d = keep.tile([P, PACK, U], F32, name="qi_d")
+        for t in range(PACK):
+            nc.vector.tensor_tensor(qi_d[:, t, :], chg[t][:].indirect(pi_sb[:]), inv_d[:, t, :], ALU.mult)
+
+        tail = keep.tile([P, PACK, S], F32, name="tail")
+        for t in range(PACK):
+            nc.scalar.activation(tail[:, t, :], pol_banks[t][:], ACT.Abs)
+        nc.scalar.activation(tail[:], tail[:], ACT.Exp, scale=-1.0)
+        for t in range(PACK):
+            nc.scalar.activation(tail[:, t, :], tail[:, t, :], ACT.Ln, bias=1.0)
+
+        factor = [gauss[:, :, : U // 2], tail]
+
+        def damped(t, h):
+            cols = slice(h * (U // 2), (h + 1) * (U // 2))
+            nc.vector.scalar_tensor_tensor(
+                factor[h][:, t, :], qi_d[:, t, cols], unit_sb[:, t : t + 1], gauss[:, t, cols], ALU.mult, ALU.mult
+            )
+
+        w3_grouped = keep.tile([P, N, PACK], BF16, name="w3_grouped", align_bytes=64)
+        w3_codes = keep.tile([P, N], U32, name="w3_codes", align_bytes=64)
+        w3_scales = keep.tile([P, N], U8, name="w3_scales", align_bytes=64)
+        nc.vector.tensor_copy(
+            w3_grouped[:].rearrange("p (c i) j -> p c j i", i=4),
+            w3_raw[:].rearrange("p j (c i) -> p c j i", i=4),
+        )
+        for t in range(PACK):
+            damped(t, 0)
+        nc.vector.quantize_mx(
+            out=w3_codes[:].bitcast(FP8X4), scales=w3_scales[:], in_=w3_grouped[:].rearrange("p c j -> p (c j)")
+        )
+        alpha = []
+        for t in range(PACK):
+            alpha_t = keep.tile([P, S], F32, name="alpha%d" % t)
+            nc.vector.scalar_tensor_tensor(alpha_t[:], pol_banks[t][:], 0.0, tail[:, t, :], ALU.max, ALU.add)
+            alpha.append(alpha_t)
+
+        starts = [sum(CHUNKS[:c]) for c in range(len(CHUNKS))]
+        widest = max(CHUNKS)
+        pair_bufs = [keep.tile([P, PACK * widest], F32, name="pair%d" % i) for i in range(len(CHUNKS) + 2)]
+        qj_first = keep.tile([P, PACK, CHUNKS[0]], F32, name="qj_first")
+
+        def view(buf, c):
+            return buf[:, : PACK * CHUNKS[c]].rearrange("p (t r) -> p t r", t=PACK)
+
+        def offsets(lst, c):
+            return lst[:, starts[c] // 16 : (starts[c] + CHUNKS[c]) // 16]
+
+        al_i = [view(pair_bufs[c], c) for c in range(2)] + [
+            qi_d[:, :, starts[c - 2] : starts[c - 2] + CHUNKS[c]] for c in range(2, len(CHUNKS))
+        ]
+        al_ij = [view(pair_bufs[c + 2], c) for c in range(len(CHUNKS))]
+        mix = al_i
+        qj = [qj_first[:]] + al_ij[1:-1] + [al_i[1]]
+
+        def fetch_alpha_i(c):
+            for t in range(PACK):
+                nc.scalar.activation(al_i[c][:, t, :], alpha[t][:].indirect(offsets(pi_sb, c)), ACT.Copy)
+
+        def fetch_qj(c):
+            for t in range(PACK):
+                nc.scalar.activation(qj[c][:, t, :], chg[t][:].indirect(offsets(pj_sb, c)), ACT.Copy)
+
+        def mix_alpha(c, t):
+            nc.vector.tensor_tensor(
+                al_ij[c][:, t, :], alpha[t][:].indirect(offsets(pj_sb, c)), al_i[c][:, t, :], ALU.mult
+            )
+
+        def root(c):
+            nc.scalar.activation(mix[c], al_ij[c], ACT.Sqrt, scale=0.25, bias=0.025)
+
+        def induced(c, lo, hi):
+            nc.vector.tensor_tensor(
+                mix[c][:, :, lo:hi], mix[c][:, :, lo:hi], qi_d[:, :, starts[c] + lo : starts[c] + hi], ALU.mult
+            )
+
+        def bracket(c, lo, hi):
+            nc.vector.tensor_tensor(mix[c][:, :, lo:hi], qj[c][:, :, lo:hi], mix[c][:, :, lo:hi], ALU.subtract)
+
+        def hidden(c, lo, hi):
+            c0 = starts[c] + lo
+            hid = ring.tile([P, hi - lo, PACK], BF16, name="hid", tag="hid", align_bytes=64)
+            nc.vector.tensor_tensor(
+                hid[:].rearrange("p (c i) t -> p c t i", i=4),
+                factor[c0 // S][:, :, c0 % S : c0 % S + hi - lo].rearrange("p t (c i) -> p c t i", i=4),
+                mix[c][:, :, lo:hi].rearrange("p t (c i) -> p c t i", i=4),
+                ALU.mult,
+            )
+            return hid
+
+        def observe(hid, c0):
+            width = hid[:].shape[1]
+            hid_codes = ring.tile([P, width], U32, name="hid_codes", tag="hid_codes", align_bytes=64)
+            hid_scales = ring.tile([P, width], U8, name="hid_scales", tag="hid_scales", align_bytes=64)
+            nc.vector.quantize_mx(
+                out=hid_codes[:].bitcast(FP8X4), scales=hid_scales[:], in_=hid[:].rearrange("p c t -> p (c t)")
+            )
+            bank = psum.tile([P, width], F32, name="out_bank", tag="w1_bank")
+            nc.tensor.matmul_mx(
+                out=bank[:],
+                lhsT=w3_codes[:].bitcast(FP8X4),
+                lhsT_scale=w3_scales[:],
+                rhs=hid_codes[:].bitcast(FP8X4),
+                rhs_scale=hid_scales[:],
+                start=True,
+                stop=True,
+            )
+            result = ring.tile([P, width], F32, name="result", tag="result")
+            nc.scalar.copy(result[:], bank[:])
+            nc.sync.dma_start(out=out[:, c0 : c0 + width], in_=result[:])
+
+        last = len(CHUNKS) - 1
+        fetch_qj(0)
+        fetch_alpha_i(0)
+        fetch_alpha_i(1)
+        for t in range(PACK):
+            mix_alpha(0, t)
+        for t in range(PACK):
+            damped(t, 1)
+        hid = None
+        for c in range(last):
+            width = CHUNKS[c]
+            root(c)
+            if c > 0:
+                fetch_qj(c)
+            mix_alpha(c + 1, 0)
+            if c > 0:
+                observe(hid, starts[c - 1])
+            mix_alpha(c + 1, 1)
+            induced(c, 0, width)
+            if c + 2 <= last:
+                fetch_alpha_i(c + 2)
+            mix_alpha(c + 1, 2)
+            bracket(c, 0, width)
+            mix_alpha(c + 1, 3)
+            hid = hidden(c, 0, width)
+        fetch_qj(last)
+        root(last)
+        half = CHUNKS[last] // 2
+        induced(last, 0, half)
+        observe(hid, starts[last - 1])
+        induced(last, half, 2 * half)
+        bracket(last, 0, half)
+        bracket(last, half, 2 * half)
+        hid_a = hidden(last, 0, half)
+        hid_b = hidden(last, half, 2 * half)
+        observe(hid_a, starts[last])
+        observe(hid_b, starts[last] + half)

@@ -17,7 +17,8 @@ ALU = mybir.AluOpType
 
 P = 128
 PACK = 4
-CHUNKS = (256, 256, 256, 256)
+CHUNKS = (256, 256, 256, 128, 128)
+FUSED = 512
 WINDOW = U + 32
 
 
@@ -27,7 +28,7 @@ def tile_picked_yewald_pol_p_kernel(
     nc = tc.nc
     with ExitStack() as ctx:
         keep = ctx.enter_context(tc.tile_pool(name="keep", bufs=1))
-        ring = ctx.enter_context(tc.tile_pool(name="ring", bufs=3))
+        ring = ctx.enter_context(tc.tile_pool(name="ring", bufs=5))
         psum = ctx.enter_context(tc.psum_pool(name="psum", bufs=4))
 
         offs_sb = keep.tile([P, S // 16], U16, name="offs_sb")
@@ -97,11 +98,13 @@ def tile_picked_yewald_pol_p_kernel(
             banks = []
             for t in range(PACK):
                 cols = slice(t * P, (t + 1) * P)
-                nc.vector.quantize_mx(
-                    out=codes[:, cols].bitcast(FP8X4),
-                    scales=scales[:, cols],
-                    in_=grouped[:, t, :, :].rearrange("p m j -> p (m j)"),
-                )
+                if t % 2 == 0:
+                    both = slice(t * P, (t + 2) * P)
+                    nc.vector.quantize_mx(
+                        out=codes[:, both].bitcast(FP8X4),
+                        scales=scales[:, both],
+                        in_=grouped[:, t : t + 2, :, :].rearrange("p t m j -> p (t m j)"),
+                    )
                 bank = psum.tile([P, S], F32, name=name + "_bank", tag=name + "_bank")
                 nc.tensor.matmul_mx(
                     out=bank[:],
@@ -123,27 +126,28 @@ def tile_picked_yewald_pol_p_kernel(
             chg.append(chg_t)
         pol_banks = product(w2_raw, "w2")
 
-        for h in range(2):
+        def gaussian(h):
             part = gauss[:, :, h * (U // 2) : (h + 1) * (U // 2)]
             nc.scalar.activation(part, part, ACT.Exp, scale=-0.64)
 
+        gaussian(0)
+
         qi_d = keep.tile([P, PACK, U], F32, name="qi_d")
-        for t in range(PACK):
+        for t in (0, 2, 3, 1):
             nc.vector.tensor_tensor(qi_d[:, t, :], chg[t][:].indirect(pi_sb[:]), inv_d[:, t, :], ALU.mult)
 
-        tail = keep.tile([P, PACK, S], F32, name="tail")
+        factor = keep.tile([P, PACK, U], F32, name="factor")
+        tail = factor[:, 2:4, :].rearrange("p a (b s) -> p (a b) s", s=S)
         for t in range(PACK):
             nc.scalar.activation(tail[:, t, :], pol_banks[t][:], ACT.Abs)
-        nc.scalar.activation(tail[:], tail[:], ACT.Exp, scale=-1.0)
+        gaussian(1)
+        nc.scalar.activation(tail, tail, ACT.Exp, scale=-1.0)
         for t in range(PACK):
             nc.scalar.activation(tail[:, t, :], tail[:, t, :], ACT.Ln, bias=1.0)
 
-        factor = [gauss[:, :, : U // 2], tail]
-
-        def damped(t, h):
-            cols = slice(h * (U // 2), (h + 1) * (U // 2))
+        def damped(t):
             nc.vector.scalar_tensor_tensor(
-                factor[h][:, t, :], qi_d[:, t, cols], unit_sb[:, t : t + 1], gauss[:, t, cols], ALU.mult, ALU.mult
+                factor[:, t, :], qi_d[:, t, :], unit_sb[:, t : t + 1], gauss[:, t, :], ALU.mult, ALU.mult
             )
 
         w3_grouped = keep.tile([P, N, PACK], BF16, name="w3_grouped", align_bytes=64)
@@ -153,66 +157,58 @@ def tile_picked_yewald_pol_p_kernel(
             w3_grouped[:].rearrange("p (c i) j -> p c j i", i=4),
             w3_raw[:].rearrange("p j (c i) -> p c j i", i=4),
         )
-        for t in range(PACK):
-            damped(t, 0)
+        damped(0)
+        damped(1)
         nc.vector.quantize_mx(
             out=w3_codes[:].bitcast(FP8X4), scales=w3_scales[:], in_=w3_grouped[:].rearrange("p c j -> p (c j)")
         )
         alpha = []
         for t in range(PACK):
-            alpha_t = keep.tile([P, S], F32, name="alpha%d" % t)
-            nc.vector.scalar_tensor_tensor(alpha_t[:], pol_banks[t][:], 0.0, tail[:, t, :], ALU.max, ALU.add)
+            alpha_t = keep.tile([P, WINDOW], F32, name="alpha%d" % t)
+            nc.vector.scalar_tensor_tensor(alpha_t[:, :S], pol_banks[t][:], 0.0, tail[:, t, :], ALU.max, ALU.add)
             alpha.append(alpha_t)
 
-        starts = [sum(CHUNKS[:c]) for c in range(len(CHUNKS))]
-        widest = max(CHUNKS)
-        pair_bufs = [keep.tile([P, PACK * widest], F32, name="pair%d" % i) for i in range(len(CHUNKS) + 2)]
-        qj_first = keep.tile([P, PACK, CHUNKS[0]], F32, name="qj_first")
+        bracket = keep.tile([P, PACK, U // 2], F32, name="bracket")
+        al_i = [keep.tile([P, U], F32, name="al_i%d" % t) for t in range(PACK)]
+        al_ij = [keep.tile([P, U], F32, name="al_ij%d" % t) for t in range(PACK)]
+        halves = [slice(0, U // 2), slice(U // 2, U)]
+        qj = [[al_ij[2 * h + t // 2][:, halves[t % 2]] for t in range(PACK)] for h in range(2)]
+        induced = al_i
 
-        def view(buf, c):
-            return buf[:, : PACK * CHUNKS[c]].rearrange("p (t r) -> p t r", t=PACK)
+        def fetch_alpha_i(t):
+            nc.scalar.activation(al_i[t][:], alpha[t][:].indirect(pi_sb[:]), ACT.Copy)
 
-        def offsets(lst, c):
-            return lst[:, starts[c] // 16 : (starts[c] + CHUNKS[c]) // 16]
+        def listed(lst, h):
+            return lst[:, h * (U // 32) : (h + 1) * (U // 32)]
 
-        al_i = [view(pair_bufs[c], c) for c in range(2)] + [
-            qi_d[:, :, starts[c - 2] : starts[c - 2] + CHUNKS[c]] for c in range(2, len(CHUNKS))
-        ]
-        al_ij = [view(pair_bufs[c + 2], c) for c in range(len(CHUNKS))]
-        mix = al_i
-        qj = [qj_first[:]] + al_ij[1:-1] + [al_i[1]]
+        def fetch_qj(t, h):
+            nc.scalar.activation(qj[h][t], chg[t][:].indirect(listed(pj_sb, h)), ACT.Copy)
 
-        def fetch_alpha_i(c):
-            for t in range(PACK):
-                nc.scalar.activation(al_i[c][:, t, :], alpha[t][:].indirect(offsets(pi_sb, c)), ACT.Copy)
+        def mix_alpha(t):
+            nc.vector.tensor_tensor(al_ij[t][:], alpha[t][:].indirect(pj_sb[:]), al_i[t][:], ALU.mult)
 
-        def fetch_qj(c):
-            for t in range(PACK):
-                nc.scalar.activation(qj[c][:, t, :], chg[t][:].indirect(offsets(pj_sb, c)), ACT.Copy)
+        def root(t):
+            nc.scalar.activation(induced[t][:], al_ij[t][:], ACT.Sqrt, scale=0.25, bias=0.025)
 
-        def mix_alpha(c, t):
+        def induce(t):
+            nc.vector.tensor_tensor(induced[t][:], induced[t][:], qi_d[:, t, :], ALU.mult)
+
+        def subtract(t, h):
+            cols = halves[h]
+            nc.vector.tensor_tensor(bracket[:, t, :], qj[h][t], induced[t][:, cols], ALU.subtract)
+
+        def subtract_fused(t, h):
+            cols = halves[h]
             nc.vector.tensor_tensor(
-                al_ij[c][:, t, :], alpha[t][:].indirect(offsets(pj_sb, c)), al_i[c][:, t, :], ALU.mult
+                bracket[:, t, :], chg[t][:].indirect(listed(pj_sb, h)), induced[t][:, cols], ALU.subtract
             )
 
-        def root(c):
-            nc.scalar.activation(mix[c], al_ij[c], ACT.Sqrt, scale=0.25, bias=0.025)
-
-        def induced(c, lo, hi):
-            nc.vector.tensor_tensor(
-                mix[c][:, :, lo:hi], mix[c][:, :, lo:hi], qi_d[:, :, starts[c] + lo : starts[c] + hi], ALU.mult
-            )
-
-        def bracket(c, lo, hi):
-            nc.vector.tensor_tensor(mix[c][:, :, lo:hi], qj[c][:, :, lo:hi], mix[c][:, :, lo:hi], ALU.subtract)
-
-        def hidden(c, lo, hi):
-            c0 = starts[c] + lo
-            hid = ring.tile([P, hi - lo, PACK], BF16, name="hid", tag="hid", align_bytes=64)
+        def hidden(c0, width):
+            hid = ring.tile([P, width, PACK], BF16, name="hid", tag="hid", align_bytes=64)
             nc.vector.tensor_tensor(
                 hid[:].rearrange("p (c i) t -> p c t i", i=4),
-                factor[c0 // S][:, :, c0 % S : c0 % S + hi - lo].rearrange("p t (c i) -> p c t i", i=4),
-                mix[c][:, :, lo:hi].rearrange("p t (c i) -> p c t i", i=4),
+                factor[:, :, c0 : c0 + width].rearrange("p t (c i) -> p c t i", i=4),
+                bracket[:, :, c0 % S : c0 % S + width].rearrange("p t (c i) -> p c t i", i=4),
                 ALU.mult,
             )
             return hid
@@ -238,40 +234,34 @@ def tile_picked_yewald_pol_p_kernel(
             nc.scalar.copy(result[:], bank[:])
             nc.sync.dma_start(out=out[:, c0 : c0 + width], in_=result[:])
 
-        last = len(CHUNKS) - 1
-        fetch_qj(0)
-        fetch_alpha_i(0)
-        fetch_alpha_i(1)
+        fused = [(3, 0)]
         for t in range(PACK):
-            mix_alpha(0, t)
+            fetch_alpha_i(t)
+        damped(2)
+        mix_alpha(0)
+        damped(3)
+        for t in range(1, PACK):
+            mix_alpha(t)
         for t in range(PACK):
-            damped(t, 1)
-        hid = None
-        for c in range(last):
-            width = CHUNKS[c]
-            root(c)
-            if c > 0:
-                fetch_qj(c)
-            mix_alpha(c + 1, 0)
-            if c > 0:
-                observe(hid, starts[c - 1])
-            mix_alpha(c + 1, 1)
-            induced(c, 0, width)
-            if c + 2 <= last:
-                fetch_alpha_i(c + 2)
-            mix_alpha(c + 1, 2)
-            bracket(c, 0, width)
-            mix_alpha(c + 1, 3)
-            hid = hidden(c, 0, width)
-        fetch_qj(last)
-        root(last)
-        half = CHUNKS[last] // 2
-        induced(last, 0, half)
-        observe(hid, starts[last - 1])
-        induced(last, half, 2 * half)
-        bracket(last, 0, half)
-        bracket(last, half, 2 * half)
-        hid_a = hidden(last, 0, half)
-        hid_b = hidden(last, half, 2 * half)
-        observe(hid_a, starts[last])
-        observe(hid_b, starts[last] + half)
+            root(t)
+            induce(t)
+        for h in range(2):
+            for t in range(PACK):
+                if (t, h) not in fused:
+                    fetch_qj(t, h)
+        waiting = None
+        c0 = 0
+        for width in CHUNKS:
+            if c0 % S == 0:
+                for t in range(PACK):
+                    if (t, c0 // S) in fused:
+                        subtract_fused(t, c0 // S)
+                for t in range(PACK):
+                    if (t, c0 // S) not in fused:
+                        subtract(t, c0 // S)
+            hid = hidden(c0, width)
+            if waiting is not None:
+                observe(*waiting)
+            waiting = (hid, c0)
+            c0 += width
+        observe(*waiting)

@@ -57,23 +57,18 @@ def tile_picked_yewald_pol_p_kernel(
         )
         nc.sync.dma_start(offs_sb[:], offs)
 
-        def load_halves(w, name):
-            rows = w.rearrange("(p j) c -> p j c", j=PACK)
-            halves = []
-            for h in range(2):
-                raw = keep.tile([P, PACK, H // 2], F32, name="%s_raw%d" % (name, h))
-                nc.sync.dma_start(out=raw[:], in_=rows[:, :, h * (H // 2) : (h + 1) * (H // 2)])
-                halves.append(raw)
-            return halves
+        def load_rows(w, name):
+            raw = keep.tile([P, PACK, w.shape[1]], F32, name=name + "_raw")
+            nc.sync.dma_start(out=raw[:], in_=w.rearrange("(p j) c -> p j c", j=PACK))
+            return raw
 
-        w1_raw = load_halves(w1, "w1")
+        w1_raw = load_rows(w1, "w1")
+        w2_raw = load_rows(w2, "w2")
+        w3_raw = load_rows(w3, "w3")
         nc.sync.dma_start(pi_sb[:], pi)
-        w2_raw = load_halves(w2, "w2")
-        nc.sync.dma_start(pj_sb[:], pj)
         unit_sb = keep.tile([P, PACK], F32, name="unit_sb")
         nc.sync.dma_start(out=unit_sb[:], in_=unit.rearrange("(p t) o -> p (t o)", t=PACK))
-        w3_raw = keep.tile([P, PACK, N], F32, name="w3_raw")
-        nc.sync.dma_start(out=w3_raw[:], in_=w3.rearrange("(p j) c -> p j c", j=PACK))
+        nc.sync.dma_start(pj_sb[:], pj)
 
         gauss = keep.tile([P, PACK, U], F32, name="gauss")
         inv_d = keep.tile([P, PACK, U], F32, name="inv_d")
@@ -86,15 +81,14 @@ def tile_picked_yewald_pol_p_kernel(
         nc.vector.tensor_copy(x_codes[:], table_words[:].indirect(offs_sb[:]))
         nc.vector.tensor_copy(x_sc[:], table_scales[:].indirect(offs_sb[:]))
 
-        def product(halves, name):
+        def product(raw, name):
             grouped = keep.tile([P, PACK, P, PACK], BF16, name=name + "_grouped", align_bytes=64)
             codes = keep.tile([P, H], U32, name=name + "_codes", align_bytes=64)
             scales = keep.tile([P, H], U8, name=name + "_scales", align_bytes=64)
-            for h in range(2):
-                nc.vector.tensor_copy(
-                    grouped[:, :, h * (P // 2) : (h + 1) * (P // 2), :].rearrange("p t m j -> p m j t"),
-                    halves[h][:].rearrange("p j (m t) -> p m j t", t=PACK),
-                )
+            nc.vector.tensor_copy(
+                grouped[:].rearrange("p t m j -> p m j t"),
+                raw[:].rearrange("p j (m t) -> p m j t", t=PACK),
+            )
             banks = []
             for t in range(PACK):
                 cols = slice(t * P, (t + 1) * P)

@@ -20,6 +20,8 @@ PACK = 4
 CHUNKS = (256, 256, 256, 128, 128)
 FUSED = 512
 WINDOW = U + 32
+EXP_SPLIT = 704
+ORDER = (0, 2, 3, 1)
 
 
 def tile_picked_yewald_pol_p_kernel(
@@ -70,11 +72,13 @@ def tile_picked_yewald_pol_p_kernel(
         nc.sync.dma_start(out=unit_sb[:], in_=unit.rearrange("(p t) o -> p (t o)", t=PACK))
         nc.sync.dma_start(pj_sb[:], pj)
 
+        halves = [slice(0, U // 2), slice(U // 2, U)]
         gauss = keep.tile([P, PACK, U], F32, name="gauss")
         inv_d = keep.tile([P, PACK, U], F32, name="inv_d")
         for t in range(PACK):
-            nc.vector.tensor_tensor(gauss[:, t, :], d[t][:], d[t][:], ALU.mult)
-            nc.scalar.activation(inv_d[:, t, :], gauss[:, t, :], ACT.Abs_reciprocal_sqrt)
+            for cols in halves:
+                nc.vector.tensor_tensor(gauss[:, t, cols], d[t][:, cols], d[t][:, cols], ALU.mult)
+                nc.scalar.activation(inv_d[:, t, cols], gauss[:, t, cols], ACT.Abs_reciprocal_sqrt)
 
         x_codes = keep.tile([P, S], U32, name="x_codes", align_bytes=64)
         x_sc = keep.tile([P, S], U8, name="x_sc", align_bytes=64)
@@ -113,21 +117,19 @@ def tile_picked_yewald_pol_p_kernel(
             return banks
 
         chg_banks = product(w1_raw, "w1")
-        chg = []
-        for t in range(PACK):
-            chg_t = keep.tile([P, WINDOW], F32, name="chg%d" % t)
-            nc.scalar.copy(chg_t[:, :S], chg_banks[t][:])
-            chg.append(chg_t)
+        chg = [keep.tile([P, WINDOW], F32, name="chg%d" % t) for t in range(PACK)]
+        for t in ORDER:
+            nc.scalar.copy(chg[t][:, :S], chg_banks[t][:])
         pol_banks = product(w2_raw, "w2")
 
         def gaussian(h):
-            part = gauss[:, :, h * (U // 2) : (h + 1) * (U // 2)]
+            part = gauss[:, :, (slice(0, EXP_SPLIT), slice(EXP_SPLIT, U))[h]]
             nc.scalar.activation(part, part, ACT.Exp, scale=-0.64)
 
         gaussian(0)
 
         qi_d = keep.tile([P, PACK, U], F32, name="qi_d")
-        for t in (0, 2, 3, 1):
+        for t in ORDER:
             nc.vector.tensor_tensor(qi_d[:, t, :], chg[t][:].indirect(pi_sb[:]), inv_d[:, t, :], ALU.mult)
 
         factor = keep.tile([P, PACK, U], F32, name="factor")
@@ -152,7 +154,7 @@ def tile_picked_yewald_pol_p_kernel(
             w3_raw[:].rearrange("p j (c i) -> p c j i", i=4),
         )
         damped(0)
-        damped(1)
+        nc.gpsimd.tensor_tensor(factor[:, 1, :], qi_d[:, 1, :], gauss[:, 1, :], ALU.mult)
         nc.vector.quantize_mx(
             out=w3_codes[:].bitcast(FP8X4), scales=w3_scales[:], in_=w3_grouped[:].rearrange("p c j -> p (c j)")
         )
@@ -165,12 +167,15 @@ def tile_picked_yewald_pol_p_kernel(
         bracket = keep.tile([P, PACK, U // 2], F32, name="bracket")
         al_i = [keep.tile([P, U], F32, name="al_i%d" % t) for t in range(PACK)]
         al_ij = [keep.tile([P, U], F32, name="al_ij%d" % t) for t in range(PACK)]
-        halves = [slice(0, U // 2), slice(U // 2, U)]
         qj = [[al_ij[2 * h + t // 2][:, halves[t % 2]] for t in range(PACK)] for h in range(2)]
         induced = al_i
 
         def fetch_alpha_i(t):
-            nc.scalar.activation(al_i[t][:], alpha[t][:].indirect(pi_sb[:]), ACT.Copy)
+            if t == 0:
+                for h in range(2):
+                    nc.scalar.activation(al_i[t][:, halves[h]], alpha[t][:].indirect(listed(pi_sb, h)), ACT.Copy)
+            else:
+                nc.scalar.activation(al_i[t][:], alpha[t][:].indirect(pi_sb[:]), ACT.Copy)
 
         def listed(lst, h):
             return lst[:, h * (U // 32) : (h + 1) * (U // 32)]
@@ -179,17 +184,33 @@ def tile_picked_yewald_pol_p_kernel(
             nc.scalar.activation(qj[h][t], chg[t][:].indirect(listed(pj_sb, h)), ACT.Copy)
 
         def mix_alpha(t):
-            nc.vector.tensor_tensor(al_ij[t][:], alpha[t][:].indirect(pj_sb[:]), al_i[t][:], ALU.mult)
+            if t == 0:
+                for h in range(2):
+                    nc.vector.tensor_tensor(
+                        al_ij[t][:, halves[h]], alpha[t][:].indirect(listed(pj_sb, h)), al_i[t][:, halves[h]], ALU.mult
+                    )
+            else:
+                nc.vector.tensor_tensor(al_ij[t][:], alpha[t][:].indirect(pj_sb[:]), al_i[t][:], ALU.mult)
 
         def root(t):
             nc.scalar.activation(induced[t][:], al_ij[t][:], ACT.Sqrt, scale=0.25, bias=0.025)
 
         def induce(t):
-            nc.vector.tensor_tensor(induced[t][:], induced[t][:], qi_d[:, t, :], ALU.mult)
+            if t == 1:
+                nc.vector.scalar_tensor_tensor(
+                    induced[t][:], induced[t][:], unit_sb[:, t : t + 1], qi_d[:, t, :], ALU.mult, ALU.mult
+                )
+            else:
+                nc.vector.tensor_tensor(induced[t][:], induced[t][:], qi_d[:, t, :], ALU.mult)
 
         def subtract(t, h):
             cols = halves[h]
-            nc.vector.tensor_tensor(bracket[:, t, :], qj[h][t], induced[t][:, cols], ALU.subtract)
+            if t == 1:
+                nc.vector.scalar_tensor_tensor(
+                    bracket[:, t, :], qj[h][t], unit_sb[:, t : t + 1], induced[t][:, cols], ALU.mult, ALU.subtract
+                )
+            else:
+                nc.vector.tensor_tensor(bracket[:, t, :], qj[h][t], induced[t][:, cols], ALU.subtract)
 
         def subtract_fused(t, h):
             cols = halves[h]

@@ -17,11 +17,16 @@ ALU = mybir.AluOpType
 
 P = 128
 PACK = 4
-CHUNKS = (256, 256, 256, 128, 128)
-FUSED = 512
+HALF = U // 2
+HALVES = (slice(0, HALF), slice(HALF, U))
 WINDOW = U + 32
+CHUNKS = (256, 256, 256, 128, 128)
 EXP_SPLIT = 704
-ORDER = (0, 2, 3, 1)
+LAST_TILE = 1
+ORDER = (0, 2, 3, LAST_TILE)
+LATE_UNIT = 2
+FUSED = (3, 0)
+CUT = (2, 0)
 
 
 def tile_picked_yewald_pol_p_kernel(
@@ -30,12 +35,15 @@ def tile_picked_yewald_pol_p_kernel(
     nc = tc.nc
     with ExitStack() as ctx:
         keep = ctx.enter_context(tc.tile_pool(name="keep", bufs=1))
-        ring = ctx.enter_context(tc.tile_pool(name="ring", bufs=5))
-        psum = ctx.enter_context(tc.psum_pool(name="psum", bufs=4))
+        ring = ctx.enter_context(tc.tile_pool(name="ring", bufs=len(CHUNKS)))
+        psum = ctx.enter_context(tc.psum_pool(name="psum", bufs=PACK))
 
         offs_sb = keep.tile([P, S // 16], U16, name="offs_sb")
         pi_sb = keep.tile([P, U // 16], U16, name="pi_sb")
         pj_sb = keep.tile([P, U // 16], U16, name="pj_sb")
+
+        def half_list(list_sb, h):
+            return list_sb[:, h * (HALF // 16) : (h + 1) * (HALF // 16)]
 
         table_scales = keep.tile([P, T], U8, name="table_scales", align_bytes=64)
         nc.vector.memset(table_scales[:].bitcast(I32), 0)
@@ -72,11 +80,10 @@ def tile_picked_yewald_pol_p_kernel(
         nc.sync.dma_start(out=unit_sb[:], in_=unit.rearrange("(p t) o -> p (t o)", t=PACK))
         nc.sync.dma_start(pj_sb[:], pj)
 
-        halves = [slice(0, U // 2), slice(U // 2, U)]
         gauss = keep.tile([P, PACK, U], F32, name="gauss")
         inv_d = keep.tile([P, PACK, U], F32, name="inv_d")
         for t in range(PACK):
-            for cols in halves:
+            for cols in HALVES:
                 nc.vector.tensor_tensor(gauss[:, t, cols], d[t][:, cols], d[t][:, cols], ALU.mult)
                 nc.scalar.activation(inv_d[:, t, cols], gauss[:, t, cols], ACT.Abs_reciprocal_sqrt)
 
@@ -122,29 +129,30 @@ def tile_picked_yewald_pol_p_kernel(
             nc.scalar.copy(chg[t][:, :S], chg_banks[t][:])
         pol_banks = product(w2_raw, "w2")
 
-        def gaussian(h):
-            part = gauss[:, :, (slice(0, EXP_SPLIT), slice(EXP_SPLIT, U))[h]]
-            nc.scalar.activation(part, part, ACT.Exp, scale=-0.64)
+        def gaussian(cols):
+            nc.scalar.activation(gauss[:, :, cols], gauss[:, :, cols], ACT.Exp, scale=-0.64)
 
-        gaussian(0)
+        gaussian(slice(0, EXP_SPLIT))
 
         qi_d = keep.tile([P, PACK, U], F32, name="qi_d")
-        for t in ORDER:
+        for t in ORDER[:-1]:
             nc.vector.tensor_tensor(qi_d[:, t, :], chg[t][:].indirect(pi_sb[:]), inv_d[:, t, :], ALU.mult)
+        for h in range(2):
+            nc.vector.tensor_tensor(
+                qi_d[:, LAST_TILE, HALVES[h]],
+                chg[LAST_TILE][:].indirect(half_list(pi_sb, h)),
+                inv_d[:, LAST_TILE, HALVES[h]],
+                ALU.mult,
+            )
 
         factor = keep.tile([P, PACK, U], F32, name="factor")
-        tail = factor[:, 2:4, :].rearrange("p a (b s) -> p (a b) s", s=S)
+        log_term = factor[:, 2:4, :].rearrange("p a (b s) -> p (a b) s", s=S)
         for t in range(PACK):
-            nc.scalar.activation(tail[:, t, :], pol_banks[t][:], ACT.Abs)
-        gaussian(1)
-        nc.scalar.activation(tail, tail, ACT.Exp, scale=-1.0)
+            nc.scalar.activation(log_term[:, t, :], pol_banks[t][:], ACT.Abs)
+        gaussian(slice(EXP_SPLIT, U))
+        nc.scalar.activation(log_term, log_term, ACT.Exp, scale=-1.0)
         for t in range(PACK):
-            nc.scalar.activation(tail[:, t, :], tail[:, t, :], ACT.Ln, bias=1.0)
-
-        def damped(t):
-            nc.vector.scalar_tensor_tensor(
-                factor[:, t, :], qi_d[:, t, :], unit_sb[:, t : t + 1], gauss[:, t, :], ALU.mult, ALU.mult
-            )
+            nc.scalar.activation(log_term[:, t, :], log_term[:, t, :], ACT.Ln, bias=1.0)
 
         w3_grouped = keep.tile([P, N, PACK], BF16, name="w3_grouped", align_bytes=64)
         w3_codes = keep.tile([P, N], U32, name="w3_codes", align_bytes=64)
@@ -153,50 +161,42 @@ def tile_picked_yewald_pol_p_kernel(
             w3_grouped[:].rearrange("p (c i) j -> p c j i", i=4),
             w3_raw[:].rearrange("p j (c i) -> p c j i", i=4),
         )
-        damped(0)
-        nc.gpsimd.tensor_tensor(factor[:, 1, :], qi_d[:, 1, :], gauss[:, 1, :], ALU.mult)
+
+        flat = [tile[:].rearrange("p t r -> p (t r)") for tile in (factor, qi_d, gauss)]
+        nc.vector.tensor_tensor(*[ap[:, : U + HALF] for ap in flat], ALU.mult)
+        nc.gpsimd.tensor_tensor(*[ap[:, U + HALF : 2 * U] for ap in flat], ALU.mult)
         nc.vector.quantize_mx(
             out=w3_codes[:].bitcast(FP8X4), scales=w3_scales[:], in_=w3_grouped[:].rearrange("p c j -> p (c j)")
         )
         alpha = []
         for t in range(PACK):
             alpha_t = keep.tile([P, WINDOW], F32, name="alpha%d" % t)
-            nc.vector.scalar_tensor_tensor(alpha_t[:, :S], pol_banks[t][:], 0.0, tail[:, t, :], ALU.max, ALU.add)
+            nc.vector.scalar_tensor_tensor(alpha_t[:, :S], pol_banks[t][:], 0.0, log_term[:, t, :], ALU.max, ALU.add)
             alpha.append(alpha_t)
 
-        bracket = keep.tile([P, PACK, U // 2], F32, name="bracket")
+        bracket = keep.tile([P, PACK, HALF], F32, name="bracket")
         al_i = [keep.tile([P, U], F32, name="al_i%d" % t) for t in range(PACK)]
         al_ij = [keep.tile([P, U], F32, name="al_ij%d" % t) for t in range(PACK)]
-        qj = [[al_ij[2 * h + t // 2][:, halves[t % 2]] for t in range(PACK)] for h in range(2)]
+        qj = [[al_ij[2 * h + t // 2][:, HALVES[t % 2]] for t in range(PACK)] for h in range(2)]
         induced = al_i
 
-        def fetch_alpha_i(t):
+        def pieces(t):
             if t == 0:
-                for h in range(2):
-                    nc.scalar.activation(al_i[t][:, halves[h]], alpha[t][:].indirect(listed(pi_sb, h)), ACT.Copy)
-            else:
-                nc.scalar.activation(al_i[t][:], alpha[t][:].indirect(pi_sb[:]), ACT.Copy)
+                return [(HALVES[h], half_list(pi_sb, h), half_list(pj_sb, h)) for h in range(2)]
+            return [(slice(0, U), pi_sb[:], pj_sb[:])]
 
-        def listed(lst, h):
-            return lst[:, h * (U // 32) : (h + 1) * (U // 32)]
-
-        def fetch_qj(t, h):
-            nc.scalar.activation(qj[h][t], chg[t][:].indirect(listed(pj_sb, h)), ACT.Copy)
+        def scaled_factor(t):
+            nc.vector.scalar_tensor_tensor(
+                factor[:, t, :], qi_d[:, t, :], unit_sb[:, t : t + 1], gauss[:, t, :], ALU.mult, ALU.mult
+            )
 
         def mix_alpha(t):
-            if t == 0:
-                for h in range(2):
-                    nc.vector.tensor_tensor(
-                        al_ij[t][:, halves[h]], alpha[t][:].indirect(listed(pj_sb, h)), al_i[t][:, halves[h]], ALU.mult
-                    )
-            else:
-                nc.vector.tensor_tensor(al_ij[t][:], alpha[t][:].indirect(pj_sb[:]), al_i[t][:], ALU.mult)
-
-        def root(t):
-            nc.scalar.activation(induced[t][:], al_ij[t][:], ACT.Sqrt, scale=0.25, bias=0.025)
+            for cols, by_pi, by_pj in pieces(t):
+                nc.vector.tensor_tensor(al_ij[t][:, cols], alpha[t][:].indirect(by_pj), al_i[t][:, cols], ALU.mult)
 
         def induce(t):
-            if t == 1:
+            nc.scalar.activation(induced[t][:], al_ij[t][:], ACT.Sqrt, scale=0.25, bias=0.025)
+            if t < LATE_UNIT:
                 nc.vector.scalar_tensor_tensor(
                     induced[t][:], induced[t][:], unit_sb[:, t : t + 1], qi_d[:, t, :], ALU.mult, ALU.mult
                 )
@@ -204,32 +204,30 @@ def tile_picked_yewald_pol_p_kernel(
                 nc.vector.tensor_tensor(induced[t][:], induced[t][:], qi_d[:, t, :], ALU.mult)
 
         def subtract(t, h):
-            cols = halves[h]
-            if t == 1:
+            minus = induced[t][:, HALVES[h]]
+            if (t, h) == FUSED:
+                nc.vector.tensor_tensor(bracket[:, t, :], chg[t][:].indirect(half_list(pj_sb, h)), minus, ALU.subtract)
+            elif t < LATE_UNIT:
                 nc.vector.scalar_tensor_tensor(
-                    bracket[:, t, :], qj[h][t], unit_sb[:, t : t + 1], induced[t][:, cols], ALU.mult, ALU.subtract
+                    bracket[:, t, :], qj[h][t], unit_sb[:, t : t + 1], minus, ALU.mult, ALU.subtract
                 )
+            elif (t, h) == CUT:
+                for part in (slice(0, CHUNKS[0]), slice(CHUNKS[0], HALF)):
+                    nc.vector.tensor_tensor(bracket[:, t, part], qj[h][t][:, part], minus[:, part], ALU.subtract)
             else:
-                nc.vector.tensor_tensor(bracket[:, t, :], qj[h][t], induced[t][:, cols], ALU.subtract)
-
-        def subtract_fused(t, h):
-            cols = halves[h]
-            nc.vector.tensor_tensor(
-                bracket[:, t, :], chg[t][:].indirect(listed(pj_sb, h)), induced[t][:, cols], ALU.subtract
-            )
+                nc.vector.tensor_tensor(bracket[:, t, :], qj[h][t], minus, ALU.subtract)
 
         def hidden(c0, width):
             hid = ring.tile([P, width, PACK], BF16, name="hid", tag="hid", align_bytes=64)
             nc.vector.tensor_tensor(
                 hid[:].rearrange("p (c i) t -> p c t i", i=4),
                 factor[:, :, c0 : c0 + width].rearrange("p t (c i) -> p c t i", i=4),
-                bracket[:, :, c0 % S : c0 % S + width].rearrange("p t (c i) -> p c t i", i=4),
+                bracket[:, :, c0 % HALF : c0 % HALF + width].rearrange("p t (c i) -> p c t i", i=4),
                 ALU.mult,
             )
             return hid
 
-        def observe(hid, c0):
-            width = hid[:].shape[1]
+        def observe(hid, c0, width):
             hid_codes = ring.tile([P, width], U32, name="hid_codes", tag="hid_codes", align_bytes=64)
             hid_scales = ring.tile([P, width], U8, name="hid_scales", tag="hid_scales", align_bytes=64)
             nc.vector.quantize_mx(
@@ -249,34 +247,31 @@ def tile_picked_yewald_pol_p_kernel(
             nc.scalar.copy(result[:], bank[:])
             nc.sync.dma_start(out=out[:, c0 : c0 + width], in_=result[:])
 
-        fused = [(3, 0)]
         for t in range(PACK):
-            fetch_alpha_i(t)
-        damped(2)
+            for cols, by_pi, by_pj in pieces(t):
+                nc.scalar.activation(al_i[t][:, cols], alpha[t][:].indirect(by_pi), ACT.Copy)
+        scaled_factor(2)
         mix_alpha(0)
-        damped(3)
+        scaled_factor(3)
         for t in range(1, PACK):
             mix_alpha(t)
         for t in range(PACK):
-            root(t)
             induce(t)
         for h in range(2):
             for t in range(PACK):
-                if (t, h) not in fused:
-                    fetch_qj(t, h)
+                if (t, h) != FUSED:
+                    nc.scalar.activation(qj[h][t], chg[t][:].indirect(half_list(pj_sb, h)), ACT.Copy)
+
         waiting = None
         c0 = 0
         for width in CHUNKS:
-            if c0 % S == 0:
-                for t in range(PACK):
-                    if (t, c0 // S) in fused:
-                        subtract_fused(t, c0 // S)
-                for t in range(PACK):
-                    if (t, c0 // S) not in fused:
-                        subtract(t, c0 // S)
+            if c0 % HALF == 0:
+                h = c0 // HALF
+                for t in sorted(range(PACK), key=lambda t: (t, h) != FUSED):
+                    subtract(t, h)
             hid = hidden(c0, width)
             if waiting is not None:
                 observe(*waiting)
-            waiting = (hid, c0)
+            waiting = (hid, c0, width)
             c0 += width
         observe(*waiting)

from contextlib import ExitStack

import concourse.mybir as mybir

K, T, S, N, H, U = 512, 1024, 512, 128, 512, 1024
FLOPS = 2 * K * H * S * 2 + 2 * H * N * U

F32 = mybir.dt.float32
BF16 = mybir.dt.bfloat16
I32 = mybir.dt.int32
U32 = mybir.dt.uint32
U16 = mybir.dt.uint16
U8 = mybir.dt.uint8
FP8X4 = mybir.dt.float8_e4m3fn_x4
ACT = mybir.ActivationFunctionType
ALU = mybir.AluOpType

P = 128
PACK = 4
HALF = U // 2
HALVES = (slice(0, HALF), slice(HALF, U))
WINDOW = U + 32
CHUNKS = (256, 256, 256, 128, 128)
EXP_SPLIT = 704
LAST_TILE = 1
ORDER = (0, 2, 3, LAST_TILE)
LATE_UNIT = 2
FUSED = (3, 0)
CUT = (2, 0)


def tile_picked_yewald_pol_p_kernel(
    tc, x_words, x_scales, w1, w2, dist, unit, w3, offs, pi, pj, out
):
    nc = tc.nc
    with ExitStack() as ctx:
        keep = ctx.enter_context(tc.tile_pool(name="keep", bufs=1))
        ring = ctx.enter_context(tc.tile_pool(name="ring", bufs=len(CHUNKS)))
        psum = ctx.enter_context(tc.psum_pool(name="psum", bufs=PACK))

        offs_sb = keep.tile([P, S // 16], U16, name="offs_sb")
        pi_sb = keep.tile([P, U // 16], U16, name="pi_sb")
        pj_sb = keep.tile([P, U // 16], U16, name="pj_sb")

        def half_list(list_sb, h):
            return list_sb[:, h * (HALF // 16) : (h + 1) * (HALF // 16)]

        table_scales = keep.tile([P, T], U8, name="table_scales", align_bytes=64)
        nc.vector.memset(table_scales[:].bitcast(I32), 0)
        for q in range(4):
            nc.scalar.dma_start(
                out=table_scales[32 * q : 32 * q + 4, :].bitcast(I32),
                in_=x_scales[0, 4 * q : 4 * q + 4, :].bitcast(I32),
            )

        dist_rows = dist.rearrange("(p t) r -> t p r", t=PACK)
        d = []
        for t in range(PACK):
            d_t = keep.tile([P, U], F32, name="d%d" % t)
            nc.sync.dma_start(out=d_t[:], in_=dist_rows[t])
            d.append(d_t)

        table_words = keep.tile([P, T], U32, name="table_words", align_bytes=64)
        nc.sync.dma_start(
            out=table_words[:].bitcast(I32),
            in_=x_words[0].rearrange("p n t -> p (n t)").bitcast(I32),
        )
        nc.sync.dma_start(offs_sb[:], offs)

        def load_rows(w, name):
            raw = keep.tile([P, PACK, w.shape[1]], F32, name=name + "_raw")
            nc.sync.dma_start(out=raw[:], in_=w.rearrange("(p j) c -> p j c", j=PACK))
            return raw

        w1_raw = load_rows(w1, "w1")
        w2_raw = load_rows(w2, "w2")
        w3_raw = load_rows(w3, "w3")
        nc.sync.dma_start(pi_sb[:], pi)
        unit_sb = keep.tile([P, PACK], F32, name="unit_sb")
        nc.sync.dma_start(out=unit_sb[:], in_=unit.rearrange("(p t) o -> p (t o)", t=PACK))
        nc.sync.dma_start(pj_sb[:], pj)

        gauss = keep.tile([P, PACK, U], F32, name="gauss")
        inv_d = keep.tile([P, PACK, U], F32, name="inv_d")
        for t in range(PACK):
            for cols in HALVES:
                nc.vector.tensor_tensor(gauss[:, t, cols], d[t][:, cols], d[t][:, cols], ALU.mult)
                nc.scalar.activation(inv_d[:, t, cols], gauss[:, t, cols], ACT.Abs_reciprocal_sqrt)

        x_codes = keep.tile([P, S], U32, name="x_codes", align_bytes=64)
        x_sc = keep.tile([P, S], U8, name="x_sc", align_bytes=64)
        nc.vector.tensor_copy(x_codes[:], table_words[:].indirect(offs_sb[:]))
        nc.vector.tensor_copy(x_sc[:], table_scales[:].indirect(offs_sb[:]))

        def product(raw, name):
            grouped = keep.tile([P, PACK, P, PACK], BF16, name=name + "_grouped", align_bytes=64)
            codes = keep.tile([P, H], U32, name=name + "_codes", align_bytes=64)
            scales = keep.tile([P, H], U8, name=name + "_scales", align_bytes=64)
            nc.vector.tensor_copy(
                grouped[:].rearrange("p t m j -> p m j t"),
                raw[:].rearrange("p j (m t) -> p m j t", t=PACK),
            )
            banks = []
            for t in range(PACK):
                cols = slice(t * P, (t + 1) * P)
                if t % 2 == 0:
                    both = slice(t * P, (t + 2) * P)
                    nc.vector.quantize_mx(
                        out=codes[:, both].bitcast(FP8X4),
                        scales=scales[:, both],
                        in_=grouped[:, t : t + 2, :, :].rearrange("p t m j -> p (t m j)"),
                    )
                bank = psum.tile([P, S], F32, name=name + "_bank", tag=name + "_bank")
                nc.tensor.matmul_mx(
                    out=bank[:],
                    lhsT=codes[:, cols].bitcast(FP8X4),
                    lhsT_scale=scales[:, cols],
                    rhs=x_codes[:].bitcast(FP8X4),
                    rhs_scale=x_sc[:],
                    start=True,
                    stop=True,
                )
                banks.append(bank)
            return banks

        chg_banks = product(w1_raw, "w1")
        chg = [keep.tile([P, WINDOW], F32, name="chg%d" % t) for t in range(PACK)]
        for t in ORDER:
            nc.scalar.copy(chg[t][:, :S], chg_banks[t][:])
        pol_banks = product(w2_raw, "w2")

        def gaussian(cols):
            nc.scalar.activation(gauss[:, :, cols], gauss[:, :, cols], ACT.Exp, scale=-0.64)

        gaussian(slice(0, EXP_SPLIT))

        qi_d = keep.tile([P, PACK, U], F32, name="qi_d")
        for t in ORDER[:-1]:
            nc.vector.tensor_tensor(qi_d[:, t, :], chg[t][:].indirect(pi_sb[:]), inv_d[:, t, :], ALU.mult)
        for h in range(2):
            nc.vector.tensor_tensor(
                qi_d[:, LAST_TILE, HALVES[h]],
                chg[LAST_TILE][:].indirect(half_list(pi_sb, h)),
                inv_d[:, LAST_TILE, HALVES[h]],
                ALU.mult,
            )

        factor = keep.tile([P, PACK, U], F32, name="factor")
        log_term = factor[:, 2:4, :].rearrange("p a (b s) -> p (a b) s", s=S)
        for t in range(PACK):
            nc.scalar.activation(log_term[:, t, :], pol_banks[t][:], ACT.Abs)
        gaussian(slice(EXP_SPLIT, U))
        nc.scalar.activation(log_term, log_term, ACT.Exp, scale=-1.0)
        for t in range(PACK):
            nc.scalar.activation(log_term[:, t, :], log_term[:, t, :], ACT.Ln, bias=1.0)

        w3_grouped = keep.tile([P, N, PACK], BF16, name="w3_grouped", align_bytes=64)
        w3_codes = keep.tile([P, N], U32, name="w3_codes", align_bytes=64)
        w3_scales = keep.tile([P, N], U8, name="w3_scales", align_bytes=64)
        nc.vector.tensor_copy(
            w3_grouped[:].rearrange("p (c i) j -> p c j i", i=4),
            w3_raw[:].rearrange("p j (c i) -> p c j i", i=4),
        )

        flat = [tile[:].rearrange("p t r -> p (t r)") for tile in (factor, qi_d, gauss)]
        nc.vector.tensor_tensor(*[ap[:, : U + HALF] for ap in flat], ALU.mult)
        nc.gpsimd.tensor_tensor(*[ap[:, U + HALF : 2 * U] for ap in flat], ALU.mult)
        nc.vector.quantize_mx(
            out=w3_codes[:].bitcast(FP8X4), scales=w3_scales[:], in_=w3_grouped[:].rearrange("p c j -> p (c j)")
        )
        alpha = []
        for t in range(PACK):
            alpha_t = keep.tile([P, WINDOW], F32, name="alpha%d" % t)
            nc.vector.scalar_tensor_tensor(alpha_t[:, :S], pol_banks[t][:], 0.0, log_term[:, t, :], ALU.max, ALU.add)
            alpha.append(alpha_t)

        bracket = keep.tile([P, PACK, HALF], F32, name="bracket")
        al_i = [keep.tile([P, U], F32, name="al_i%d" % t) for t in range(PACK)]
        al_ij = [keep.tile([P, U], F32, name="al_ij%d" % t) for t in range(PACK)]
        qj = [[al_ij[2 * h + t // 2][:, HALVES[t % 2]] for t in range(PACK)] for h in range(2)]
        induced = al_i

        def pieces(t):
            if t == 0:
                return [(HALVES[h], half_list(pi_sb, h), half_list(pj_sb, h)) for h in range(2)]
            return [(slice(0, U), pi_sb[:], pj_sb[:])]

        def scaled_factor(t):
            nc.vector.scalar_tensor_tensor(
                factor[:, t, :], qi_d[:, t, :], unit_sb[:, t : t + 1], gauss[:, t, :], ALU.mult, ALU.mult
            )

        def mix_alpha(t):
            for cols, by_pi, by_pj in pieces(t):
                nc.vector.tensor_tensor(al_ij[t][:, cols], alpha[t][:].indirect(by_pj), al_i[t][:, cols], ALU.mult)

        def induce(t):
            nc.scalar.activation(induced[t][:], al_ij[t][:], ACT.Sqrt, scale=0.25, bias=0.025)
            if t < LATE_UNIT:
                nc.vector.scalar_tensor_tensor(
                    induced[t][:], induced[t][:], unit_sb[:, t : t + 1], qi_d[:, t, :], ALU.mult, ALU.mult
                )
            else:
                nc.vector.tensor_tensor(induced[t][:], induced[t][:], qi_d[:, t, :], ALU.mult)

        def subtract(t, h):
            minus = induced[t][:, HALVES[h]]
            if (t, h) == FUSED:
                nc.vector.tensor_tensor(bracket[:, t, :], chg[t][:].indirect(half_list(pj_sb, h)), minus, ALU.subtract)
            elif t < LATE_UNIT:
                nc.vector.scalar_tensor_tensor(
                    bracket[:, t, :], qj[h][t], unit_sb[:, t : t + 1], minus, ALU.mult, ALU.subtract
                )
            elif (t, h) == CUT:
                for part in (slice(0, CHUNKS[0]), slice(CHUNKS[0], HALF)):
                    nc.vector.tensor_tensor(bracket[:, t, part], qj[h][t][:, part], minus[:, part], ALU.subtract)
            else:
                nc.vector.tensor_tensor(bracket[:, t, :], qj[h][t], minus, ALU.subtract)

        def hidden(c0, width):
            hid = ring.tile([P, width, PACK], BF16, name="hid", tag="hid", align_bytes=64)
            nc.vector.tensor_tensor(
                hid[:].rearrange("p (c i) t -> p c t i", i=4),
                factor[:, :, c0 : c0 + width].rearrange("p t (c i) -> p c t i", i=4),
                bracket[:, :, c0 % HALF : c0 % HALF + width].rearrange("p t (c i) -> p c t i", i=4),
                ALU.mult,
            )
            return hid

        def observe(hid, c0, width):
            hid_codes = ring.tile([P, width], U32, name="hid_codes", tag="hid_codes", align_bytes=64)
            hid_scales = ring.tile([P, width], U8, name="hid_scales", tag="hid_scales", align_bytes=64)
            nc.vector.quantize_mx(
                out=hid_codes[:].bitcast(FP8X4), scales=hid_scales[:], in_=hid[:].rearrange("p c t -> p (c t)")
            )
            bank = psum.tile([P, width], F32, name="out_bank", tag="w1_bank")
            nc.tensor.matmul_mx(
                out=bank[:],
                lhsT=w3_codes[:].bitcast(FP8X4),
                lhsT_scale=w3_scales[:],
                rhs=hid_codes[:].bitcast(FP8X4),
                rhs_scale=hid_scales[:],
                start=True,
                stop=True,
            )
            result = ring.tile([P, width], F32, name="result", tag="result")
            nc.scalar.copy(result[:], bank[:])
            nc.sync.dma_start(out=out[:, c0 : c0 + width], in_=result[:])

        for t in range(PACK):
            for cols, by_pi, by_pj in pieces(t):
                nc.scalar.activation(al_i[t][:, cols], alpha[t][:].indirect(by_pi), ACT.Copy)
        scaled_factor(2)
        mix_alpha(0)
        scaled_factor(3)
        for t in range(1, PACK):
            mix_alpha(t)
        for t in range(PACK):
            induce(t)
        for h in range(2):
            for t in range(PACK):
                if (t, h) != FUSED:
                    nc.scalar.activation(qj[h][t], chg[t][:].indirect(half_list(pj_sb, h)), ACT.Copy)

        waiting = None
        c0 = 0
        for width in CHUNKS:
            if c0 % HALF == 0:
                h = c0 // HALF
                for t in sorted(range(PACK), key=lambda t: (t, h) != FUSED):
                    subtract(t, h)
            hid = hidden(c0, width)
            if waiting is not None:
                observe(*waiting)
            waiting = (hid, c0, width)
            c0 += width
        observe(*waiting)
